import numpy as np, ml_dtypes
CORES = [33,161,289,417,57,185,313,441]
N = 8
import mx_ref
NC = 256
CNT = [[0,64,0,64,80,0,0,48],[8,0,112,72,24,0,40,0],[24,24,0,8,48,56,56,40],[56,8,24,56,0,80,32,0],[8,136,8,0,56,24,24,0],[56,0,8,0,8,0,48,136],[104,24,0,56,16,32,0,24],[0,0,104,0,24,64,56,8]]
OFF = [[sum(c[:e]) for e in range(N + 1)] for c in CNT]
BF = ml_dtypes.bfloat16
def setup_inputs(rng):
    def f(*shape):
        return mx_ref.flush((rng.standard_normal(shape, dtype=np.float32) * np.exp2(rng.integers(-2, 3, shape[:-1] + (1,)))).astype(BF))
    return {"w": f(N, 128, 512), "x": f(N, 128, 4 * NC)}
def setup_inputs_blocks(rng):
    d = setup_inputs(rng)
    for k in ("w", "x"): d[k] = mx_ref.spread(d[k], rng, 4)
    return d
def setup_inputs_wide(rng):
    d = setup_inputs(rng)
    for k in ("w", "x"): d[k] = mx_ref.flush((d[k].astype(np.float32) * np.exp2(rng.integers(-8, 9, (N, 1, 1))).astype(np.float32)).astype(BF))
    return d
def setup_inputs_zeros(rng):
    d = setup_inputs(rng); v = d["x"].reshape(N, 128, -1, 4).copy()
    v[np.broadcast_to((rng.random((N, 1, v.shape[2], 1)) < 0.33), v.shape)] = 0
    d["x"] = v.reshape(d["x"].shape)
    return d
def reference(w, x):
    y = np.zeros((N, 128, NC), np.float32)
    for e in range(N):
        t = np.concatenate([x[j][:, 4 * OFF[j][e]:4 * OFF[j][e + 1]] for j in range(N)], axis=1)
        p = mx_ref.matmul(mx_ref.quantize(w[e]), mx_ref.quantize(t)); c = 0
        for j in range(N):
            a, b = OFF[j][e], OFF[j][e + 1]
            y[j][:, a:b] = p[:, c:c + b - a]; c += b - a
    return {"y": y}

from concourse.bass import DstId, RemoteDMATransfer
from concourse.mybir import dt

NSIM = 512
N = 8
WC = 128
XC = 256

SCRATCH = {
    "wb": ("sbuf", [128, 4 * WC], "bfloat16"),
    "xb": ("sbuf", [128, 4 * XC], "bfloat16"),
    "wq": ("sbuf", [128, N * WC], "float8_e4m3fn_x4"),
    "ws": ("sbuf", [128, N * WC], "uint8"),
    "xq": ("sbuf", [128, XC], "float8_e4m3fn_x4"),
    "xs": ("sbuf", [128, XC], "uint8"),
    "yb": ("sbuf", [128, XC], "float32"),
    "ps": ("psum", [128, 512 * N], "float32"),
}
SEMAPHORES = (["lw", "lx", "qw", "qx", "hs", "hc", "sent", "st0", "st1"]
              + ["a%d" % e for e in range(N)] + ["mm%d" % k for k in range(N)] + ["cp%d" % k for k in range(N)])

_CACHE = {}


def _bits(m):
    return [k for k in range(m.bit_length()) if (m >> k) & 1]


def _mask(engines):
    return sum(1 << k for k in engines)


def _split(engines, parts):
    n = len(engines) // parts
    return [engines[i * n:(i + 1) * n] for i in range(parts)]


def _plan(T, topo):
    if "p" in _CACHE:
        return _CACHE["p"]
    cores = list(T.cores)
    cnt = T.tables["CNT"]
    rank = {c: i for i, c in enumerate(cores)}
    at = {(topo.host(c), topo.chip(c)): c for c in cores}
    hosts = sorted({topo.host(c) for c in cores})
    chips = sorted({topo.chip(c) for c in cores})

    roles = {}
    for r in cores:
        other = [q for q in cores if topo.host(q) == topo.host(r) and q != r][0]
        here = [c for c in range(NSIM) if c != r and topo.host(c) == topo.host(r) and topo.chip(c) == topo.chip(r)]
        may = [c for c in here if topo.may_write(c, other)]
        same = [c for c in may if topo.die(c) == topo.die(r)]
        cross = [c for c in may if topo.die(c) != topo.die(r)]
        roles[r] = {"loc": same[0], "near": same[1], "far": cross[0]}

    first = {}
    helper = {}
    arrive = {c: {} for c in cores}

    for e, s in enumerate(cores):
        h, c = topo.host(s), topo.chip(s)
        c2 = [x for x in chips if x != c][0]
        hn = [x for x in hosts if x != h and topo.rack(x) == topo.rack(h)][0]
        hf = [x for x in hosts if topo.rack(x) != topo.rack(h) and topo.may_write(s, at[(x, c)])][0]
        hd = [x for x in hosts if x not in (h, hn, hf)][0]

        def need(q):
            return cnt[rank[q]][e] > 0

        def hop(role, home, off):
            off = [q for q in off if need(q)]
            chip_rank = home if (home != s and need(home)) else None
            if off:
                return {"e": e, "to": roles[home][role], "off": off, "chip": chip_rank, "direct": False}
            if chip_rank is not None:
                return {"e": e, "to": chip_rank, "off": [], "chip": None, "direct": True}
            return None

        offs = [hop("far", at[(hf, c)], [at[(hf, c2)], at[(hd, c2)]]), hop("near", at[(hn, c)], [at[(hd, c)]])]
        offs = [x for x in offs if x is not None]
        offs.sort(key=lambda x: -len(x["off"]))
        loc = hop("loc", s, [at[(h, c2)], at[(hn, c2)]])
        first[s] = (offs, loc)

        leave = _bits(topo.mask(s, offs[0]["to"]))
        for x, eng in zip(offs, _split(leave, len(offs))):
            x["seng"], x["ceng"] = eng, leave
        if loc is not None:
            stay = _bits(topo.mask(s, loc["to"]) & ~_mask(leave))
            loc["seng"], loc["ceng"] = stay, stay
        for pos, x in [(i + 1, x) for i, x in enumerate(offs)] + ([(1, loc)] if loc is not None else []):
            if x["direct"]:
                arrive[x["to"]][e] = [len(x["seng"]) + len(x["ceng"]), pos]
                continue
            hp = x["to"]
            helper[hp] = x
            out = _bits(topo.mask(hp, x["off"][0]))
            x["fwd"] = list(zip(x["off"], _split(out, len(x["off"]))))
            for q, eng in x["fwd"]:
                arrive[q][e] = [2 * len(eng), pos + 2 + len(x["off"])]
            if x["chip"] is not None:
                x["chip_eng"] = _bits(topo.mask(hp, x["chip"]) & ~_mask(out))
                arrive[x["chip"]][e] = [2 * len(x["chip_eng"]), pos + 2.5]

    _CACHE["p"] = {"first": first, "helper": helper, "arrive": arrive}
    return _CACHE["p"]


def _send(g, T, topo, src, e, codes, dests):
    def view():
        if codes:
            return T.wq[:, e * WC:(e + 1) * WC].bitcast(dt.uint8)
        return T.ws[:, e * WC:(e + 1) * WC]
    if len(dests) == 1:
        d, eng, sem = dests[0]
        rid, pid = topo.addr(d, src)
        g.remote_dma(out_ap=view(), in_ap=view(), remote_sem=sem, local_sem=T.sem.sent, pid=pid, routing_id=rid,
                     dma_engine_mask=_mask(eng))
    else:
        trs = []
        for d, eng, sem in dests:
            rid, pid = topo.addr(d, src)
            trs.append(RemoteDMATransfer(dst_ids=[DstId(rid=rid, pnc=pid)], dma_engine_mask=_mask(eng), remote_sem=sem,
                                         src=view(), dst=view()))
        g.remote_dma_fused(trs, local_sem=T.sem.sent)
    return sum(len(eng) for _, eng, _ in dests)


def _helper(g, core, T, topo, x):
    e = x["e"]
    a = T.sem["a%d" % e]
    sent = 0
    for codes, sem, n in ((False, T.sem.hs, len(x["seng"])), (True, T.sem.hc, len(x["ceng"]))):
        g.wait_ge(sem, n)
        sent += _send(g, T, topo, core, e, codes, [(q, eng, a) for q, eng in x["fwd"]])
        if x["chip"] is not None:
            sent += _send(g, T, topo, core, e, codes, [(x["chip"], x["chip_eng"], a)])
    g.wait_ge(T.sem.sent, sent)


def _rank(g, core, T, topo, P):
    r = T.rank_of(core)
    cnt = T.tables["CNT"][r]
    S = T.sem
    own = slice(r * WC, (r + 1) * WC)

    g.sync.dma_start(T.wb[:], T.w[:]).then_inc(S.lw, 16)
    g.sync.dma_start(T.xb[:], T.x[:]).then_inc(S.lx, 16)
    g.vector.wait_ge(S.lw, 16)
    g.vector.quantize_mx(T.wq[:, own], T.ws[:, own], T.wb[:]).then_inc(S.qw, 1)
    g.vector.wait_ge(S.lx, 16)
    g.vector.quantize_mx(T.xq[:], T.xs[:], T.xb[:]).then_inc(S.qx, 1)

    offs, loc = P["first"][core]

    def sem_of(x, codes):
        if x["direct"]:
            return S["a%d" % r]
        return S.hc if codes else S.hs

    g.wait_ge(S.qw, 1)
    sent = _send(g, T, topo, core, r, False, [(x["to"], x["seng"], sem_of(x, False)) for x in offs])
    if loc is not None:
        sent += _send(g, T, topo, core, r, False, [(loc["to"], loc["seng"], sem_of(loc, False))])
    for i, x in enumerate(offs):
        sent += _send(g, T, topo, core, r, True, [(x["to"], x["ceng"], sem_of(x, True))])
        if i == 0 and loc is not None:
            sent += _send(g, T, topo, core, r, True, [(loc["to"], loc["ceng"], sem_of(loc, True))])
    g.wait_ge(S.sent, sent)

    arr = P["arrive"][core]
    order = sorted([e for e in range(N) if cnt[e] > 0], key=lambda e: (0 if e == r else arr[e][1], e))
    off = [sum(cnt[:e]) for e in range(N + 1)]
    stores = [0, 0]
    g.tensor.wait_ge(S.qx, 1)
    for k, e in enumerate(order):
        a, b = off[e], off[e + 1]
        n = max(WC, b - a)
        a0 = min(a, XC - n)
        if e == r:
            g.tensor.wait_ge(S.qw, 1)
        else:
            g.tensor.wait_ge(S["a%d" % e], arr[e][0])
        g.tensor.matmul_mx(T.ps[:, 512 * k:512 * k + n], T.wq[:, e * WC:(e + 1) * WC], T.ws[:, e * WC:(e + 1) * WC],
                           T.xq[:, a0:a0 + n], T.xs[:, a0:a0 + n], True, True).then_inc(S["mm%d" % k], 1)
        g.vector.wait_ge(S["mm%d" % k], 1)
        g.vector.tensor_copy(T.yb[:, a:b], T.ps[:, 512 * k + a - a0:512 * k + b - a0]).then_inc(S["cp%d" % k], 1)
        q = (g.sync, g.scalar)[k % 2]
        q.wait_ge(S["cp%d" % k], 1)
        q.dma_start(T.y[:, a:b], T.yb[:, a:b]).then_inc(S["st%d" % (k % 2)], 16)
        stores[k % 2] += 16
    for i, q in enumerate((g.sync, g.scalar)):
        if stores[i]:
            q.wait_ge(S["st%d" % i], stores[i])


def rank_program(g, core, T, topo):
    P = _plan(T, topo)
    if T.rank_of(core) is not None:
        _rank(g, core, T, topo, P)
    elif core in P["helper"]:
        _helper(g, core, T, topo, P["helper"][core])
